import numpy as np
CORES = [96,97,98,99,100,101,102,103,112,113,114,115,116,117,118,119]
N = 16
GROUPS = [[0,1,2,3,4,5,6,7],[8,9,10,11,12,13,14,15]]
def setup_inputs(rng):
    return {"x": rng.standard_normal((N, 128, 1024), dtype=np.float32)}
def reference(x):
    y = np.empty((N, 128, 128), x.dtype)
    for g in GROUPS:
        s = x[g].sum(axis=0, dtype=np.float64).astype(x[g].dtype)
        n = len(g); b = x.shape[2] // n
        for i, r in enumerate(g):
            y[r] = s[:, i * b:(i + 1) * b]
    return {"y": y}

@@ -1,0 +1,84 @@
+from concourse.bass import DstId, RemoteDMATransfer
+
+N = 8
+G = 2
+K = 1
+B = 128
+W = 128 // K
+RC = 128 // K
+
+SCRATCH = {
+    "xs": ("dram", [K * N, 128, W], "float32"),
+    "land": ("dram", [K * N, 128, W], "float32"),
+    "res": ("dram", [K * G, 128, W], "float32"),
+}
+SEMAPHORES = (["ld%d" % k for k in range(K)] + ["arr%d" % k for k in range(K)]
+              + ["fin%d" % k for k in range(K)] + ["snt", "st"])
+
+
+def rank_program(g, core, T, topo):
+    rank = T.rank_of(core)
+    if rank is None:
+        return
+    group = [grp for grp in T.tables["GROUPS"] if rank in grp][0]
+    i = group.index(rank)
+    cores = [T.cores[r] for r in group]
+
+    def dst(j):
+        rid, pid, _se = topo.addr(cores[j])
+        return DstId(rid=rid, pnc=pid)
+
+    queues = [g.sync, g.scalar]
+    mine = i ^ G
+    myq, mym = divmod(mine, G)
+
+    nd = 0
+    for k in range(K):
+        for q in range(N // G):
+            queues[nd % 2].dma_start(
+                T.xs[k * N + q * G:k * N + (q + 1) * G],
+                T.x[k * RC:(k + 1) * RC, q * G * B:(q + 1) * G * B],
+            ).then_inc(T.sem["ld%d" % k], 16)
+            nd += 1
+
+    for k in range(K):
+        g.wait_ge(T.sem["ld%d" % k], 16 * (N // G))
+        trs = []
+        for p in range(N):
+            if p == mine:
+                continue
+            trs.append(RemoteDMATransfer(
+                dst_ids=[dst(p ^ G)], dma_engine_mask=3 << (2 * len(trs)), remote_sem=T.sem["arr%d" % k],
+                src=T.xs[k * N + p], dst=T.land[k * N + i]))
+        g.remote_dma_fused(trs, local_sem=T.sem.snt)
+
+    for k in range(K):
+        g.wait_ge(T.sem["arr%d" % k], 2 * (N - 1))
+        srcs = [T.land[k * N + s] for s in range(N) if s != i] + [T.xs[k * N + mine]]
+        g.remote_dma_fused([RemoteDMATransfer(
+            dst_ids=[dst(myq * G + t) for t in range(G)], dma_engine_mask=0xFFFF, remote_sem=T.sem["fin%d" % k],
+            srcs=srcs, dsts=[T.res[k * G + mym] for t in range(G)], alu_op=1)], local_sem=T.sem.snt)
+
+    jj = i % G
+    ns = 0
+    for k in range(K):
+        fin = T.sem["fin%d" % k]
+        if G == 1:
+            g.sync.wait_ge(fin, 16)
+            g.sync.dma_start(T.y[k * RC:(k + 1) * RC, :], T.res[k]).then_inc(T.sem.st, 16)
+            ns += 1
+        elif K == 1:
+            g.sync.wait_ge(fin, 16 * G)
+            g.sync.dma_start(T.y[:, :], T.res[0:G, jj::G, :]).then_inc(T.sem.st, 16)
+            ns += 1
+        else:
+            for h in range(K):
+                qu = queues[h % 2]
+                if h < 2:
+                    qu.wait_ge(fin, 16 * G)
+                qu.dma_start(T.y[k * RC:(k + 1) * RC, h * W:(h + 1) * W],
+                             T.res[k * G:(k + 1) * G, jj * K + h::G * K, :]).then_inc(T.sem.st, 16)
+                ns += 1
+
+    g.wait_ge(T.sem.snt, K * (2 * (N - 1) + 16))
+    g.wait_ge(T.sem.st, 16 * ns)

@@ -2,7 +2,7 @@ from concourse.bass import DstId, RemoteDMATransfer
 
 N = 8
 G = 2
-K = 1
+K = 2
 B = 128
 W = 128 // K
 RC = 128 // K

@@ -1,7 +1,7 @@
 from concourse.bass import DstId, RemoteDMATransfer
 
 N = 8
-G = 2
+G = 1
 K = 2
 B = 128
 W = 128 // K

@@ -1,19 +1,19 @@
 from concourse.bass import DstId, RemoteDMATransfer
 
 N = 8
-G = 1
-K = 2
 B = 128
-W = 128 // K
-RC = 128 // K
+K = 2
+R = 128 // K
+ENG = 2
 
 SCRATCH = {
-    "xs": ("dram", [K * N, 128, W], "float32"),
-    "land": ("dram", [K * N, 128, W], "float32"),
-    "res": ("dram", [K * G, 128, W], "float32"),
+    "xs": ("dram", [K * N, 128, R], "float32"),
+    "own": ("dram", [K, 128, R], "float32"),
+    "land": ("dram", [K * N, 128, R], "float32"),
+    "res": ("dram", [K, 128, R], "float32"),
 }
 SEMAPHORES = (["ld%d" % k for k in range(K)] + ["arr%d" % k for k in range(K)]
-              + ["fin%d" % k for k in range(K)] + ["snt", "st"])
+              + ["fin%d" % k for k in range(K)] + ["ldo", "snt", "st"])
 
 
 def rank_program(g, core, T, topo):
@@ -29,56 +29,37 @@ def rank_program(g, core, T, topo):
         return DstId(rid=rid, pnc=pid)
 
     queues = [g.sync, g.scalar]
-    mine = i ^ G
-    myq, mym = divmod(mine, G)
+    mine = i ^ 1
+    others = [b for b in range(N) if b != mine]
 
     nd = 0
     for k in range(K):
-        for q in range(N // G):
-            queues[nd % 2].dma_start(
-                T.xs[k * N + q * G:k * N + (q + 1) * G],
-                T.x[k * RC:(k + 1) * RC, q * G * B:(q + 1) * G * B],
-            ).then_inc(T.sem["ld%d" % k], 16)
+        for b in others:
+            queues[nd % 2].dma_start(T.xs[k * N + b], T.x[k * R:(k + 1) * R, b * B:(b + 1) * B]
+                                     ).then_inc(T.sem["ld%d" % k], 16)
             nd += 1
+    queues[nd % 2].dma_start(T.own[:, :, :], T.x[:, mine * B:(mine + 1) * B]).then_inc(T.sem.ldo, 16)
 
     for k in range(K):
-        g.wait_ge(T.sem["ld%d" % k], 16 * (N // G))
+        g.wait_ge(T.sem["ld%d" % k], 16 * (N - 1))
         trs = []
-        for p in range(N):
-            if p == mine:
-                continue
+        for b in others:
             trs.append(RemoteDMATransfer(
-                dst_ids=[dst(p ^ G)], dma_engine_mask=3 << (2 * len(trs)), remote_sem=T.sem["arr%d" % k],
-                src=T.xs[k * N + p], dst=T.land[k * N + i]))
+                dst_ids=[dst(b ^ 1)], dma_engine_mask=((1 << ENG) - 1) << (ENG * len(trs)),
+                remote_sem=T.sem["arr%d" % k], src=T.xs[k * N + b], dst=T.land[k * N + i]))
         g.remote_dma_fused(trs, local_sem=T.sem.snt)
 
+    g.wait_ge(T.sem.ldo, 16)
     for k in range(K):
-        g.wait_ge(T.sem["arr%d" % k], 2 * (N - 1))
-        srcs = [T.land[k * N + s] for s in range(N) if s != i] + [T.xs[k * N + mine]]
+        g.wait_ge(T.sem["arr%d" % k], ENG * (N - 1))
+        srcs = [T.land[k * N + s] for s in range(N) if s != i] + [T.own[k]]
         g.remote_dma_fused([RemoteDMATransfer(
-            dst_ids=[dst(myq * G + t) for t in range(G)], dma_engine_mask=0xFFFF, remote_sem=T.sem["fin%d" % k],
-            srcs=srcs, dsts=[T.res[k * G + mym] for t in range(G)], alu_op=1)], local_sem=T.sem.snt)
+            dst_ids=[dst(mine)], dma_engine_mask=0xFFFF, remote_sem=T.sem["fin%d" % k],
+            srcs=srcs, dsts=[T.res[k]], alu_op=1)], local_sem=T.sem.snt)
 
-    jj = i % G
-    ns = 0
     for k in range(K):
-        fin = T.sem["fin%d" % k]
-        if G == 1:
-            g.sync.wait_ge(fin, 16)
-            g.sync.dma_start(T.y[k * RC:(k + 1) * RC, :], T.res[k]).then_inc(T.sem.st, 16)
-            ns += 1
-        elif K == 1:
-            g.sync.wait_ge(fin, 16 * G)
-            g.sync.dma_start(T.y[:, :], T.res[0:G, jj::G, :]).then_inc(T.sem.st, 16)
-            ns += 1
-        else:
-            for h in range(K):
-                qu = queues[h % 2]
-                if h < 2:
-                    qu.wait_ge(fin, 16 * G)
-                qu.dma_start(T.y[k * RC:(k + 1) * RC, h * W:(h + 1) * W],
-                             T.res[k * G:(k + 1) * G, jj * K + h::G * K, :]).then_inc(T.sem.st, 16)
-                ns += 1
+        g.sync.wait_ge(T.sem["fin%d" % k], 16)
+        g.sync.dma_start(T.y[k * R:(k + 1) * R, :], T.res[k]).then_inc(T.sem.st, 16)
 
-    g.wait_ge(T.sem.snt, K * (2 * (N - 1) + 16))
-    g.wait_ge(T.sem.st, 16 * ns)
+    g.wait_ge(T.sem.snt, K * (ENG * (N - 1) + 16))
+    g.wait_ge(T.sem.st, 16 * K)

from concourse.bass import DstId, RemoteDMATransfer

N = 8
B = 128
K = 2
R = 128 // K
ENG = 2

SCRATCH = {
    "xs": ("dram", [K * N, 128, R], "float32"),
    "own": ("dram", [K, 128, R], "float32"),
    "land": ("dram", [K * N, 128, R], "float32"),
    "res": ("dram", [K, 128, R], "float32"),
}
SEMAPHORES = (["ld%d" % k for k in range(K)] + ["arr%d" % k for k in range(K)]
              + ["fin%d" % k for k in range(K)] + ["ldo", "snt", "st"])


def rank_program(g, core, T, topo):
    rank = T.rank_of(core)
    if rank is None:
        return
    group = [grp for grp in T.tables["GROUPS"] if rank in grp][0]
    i = group.index(rank)
    cores = [T.cores[r] for r in group]

    def dst(j):
        rid, pid, _se = topo.addr(cores[j])
        return DstId(rid=rid, pnc=pid)

    queues = [g.sync, g.scalar]
    mine = i ^ 1
    others = [b for b in range(N) if b != mine]

    nd = 0
    for k in range(K):
        for b in others:
            queues[nd % 2].dma_start(T.xs[k * N + b], T.x[k * R:(k + 1) * R, b * B:(b + 1) * B]
                                     ).then_inc(T.sem["ld%d" % k], 16)
            nd += 1
    queues[nd % 2].dma_start(T.own[:, :, :], T.x[:, mine * B:(mine + 1) * B]).then_inc(T.sem.ldo, 16)

    for k in range(K):
        g.wait_ge(T.sem["ld%d" % k], 16 * (N - 1))
        trs = []
        for b in others:
            trs.append(RemoteDMATransfer(
                dst_ids=[dst(b ^ 1)], dma_engine_mask=((1 << ENG) - 1) << (ENG * len(trs)),
                remote_sem=T.sem["arr%d" % k], src=T.xs[k * N + b], dst=T.land[k * N + i]))
        g.remote_dma_fused(trs, local_sem=T.sem.snt)

    g.wait_ge(T.sem.ldo, 16)
    for k in range(K):
        g.wait_ge(T.sem["arr%d" % k], ENG * (N - 1))
        srcs = [T.land[k * N + s] for s in range(N) if s != i] + [T.own[k]]
        g.remote_dma_fused([RemoteDMATransfer(
            dst_ids=[dst(mine)], dma_engine_mask=0xFFFF, remote_sem=T.sem["fin%d" % k],
            srcs=srcs, dsts=[T.res[k]], alu_op=1)], local_sem=T.sem.snt)

    for k in range(K):
        g.sync.wait_ge(T.sem["fin%d" % k], 16)
        g.sync.dma_start(T.y[k * R:(k + 1) * R, :], T.res[k]).then_inc(T.sem.st, 16)

    g.wait_ge(T.sem.snt, K * (ENG * (N - 1) + 16))
    g.wait_ge(T.sem.st, 16 * K)
